import numpy as np, ml_dtypes
CORES = [9,10,11,14,17,18,19,22,49,50,51,54]
N = 12
V, DEP = 65536, 8
def entries(a): return a.T.reshape(-1)
def pack(v, P): return np.ascontiguousarray(np.asarray(v, np.int32).reshape(-1, P).T)
def forest(rng, n, lev):
    P = np.arange(n)
    for l in range(1, int(lev.max()) + 1):
        a, b = np.nonzero(lev == l)[0], np.nonzero(lev == l - 1)[0]; P[a] = b[rng.integers(0, len(b), len(a))]
    return P
def lists(rng, how):
    n = N * V; P = np.arange(n)
    if how == "uniform":
        lev = rng.integers(0, DEP + 1, n); lev[rng.permutation(n)[:DEP + 1]] = np.arange(DEP + 1); P = forest(rng, n, lev)
    if how == "star":
        lev = np.ones(n, np.int64); lev[rng.permutation(n)[:4]] = 0; P = forest(rng, n, lev)
    if how == "chain":
        W = np.stack([V * r + rng.permutation(V)[:V // (DEP + 1) * (DEP + 1)].reshape(-1, DEP + 1) for r in range(N)]); P[W[:, :, 1:]] = np.roll(W, 1, axis=0)[:, :, :-1]
    if how == "deep":
        z = rng.permutation(N); g = V * z[1 + np.arange(DEP) % (N - 1)] + rng.permutation(V)[:DEP]; P[:] = g[-1]; P[g] = np.concatenate([g[:1], g[:-1]])
    if how == "whole":
        o = rng.permutation(N)
        for i in range(1, N - 1):
            if i % (DEP + 1): P[V * o[i]:V * o[i] + V] = V * o[i - 1] + rng.permutation(V)
        P[V * o[-1]:V * o[-1] + V] = V * o[-1] + forest(rng, V, rng.permutation(np.concatenate([np.arange(DEP + 1), rng.integers(0, DEP + 1, V - DEP - 1)])))
    return {"par": np.stack([pack(p, 16) for p in P.reshape(N, V)])}
def setup_inputs(rng):
    return dict({"val": rng.standard_normal((N, 16, V // 16), dtype=np.float32).astype(ml_dtypes.bfloat16)}, **lists(rng, "uniform"))
def setup_inputs_chain(rng):
    d = setup_inputs(rng); d.update(lists(rng, "chain"))
    for k in ("val",): d[k] = (d[k].astype(np.float32) * 1048576.0).astype(d[k].dtype)
    return d
def setup_inputs_deep(rng):
    d = setup_inputs(rng); d.update(lists(rng, "deep"))
    for k in ("val",): d[k] = (d[k].astype(np.float32) * (1 / 1024.0)).astype(d[k].dtype)
    return d
def setup_inputs_star(rng):
    d = setup_inputs(rng); d.update(lists(rng, "star"))
    return d
def setup_inputs_whole(rng):
    d = setup_inputs(rng); d.update(lists(rng, "whole"))
    return d
def check_inputs(x):
    bad = []
    if x["par"].min() < 0 or x["par"].max() >= N * V: bad.append("par out of range")
    p = np.concatenate([entries(a) for a in x["par"]]); q = p
    for k in range(DEP - 1): q = p[q]
    if (p[q] != q).any(): bad.append("a node is more than DEP hops from a root")
    return bad
def reference(val, par):
    p = np.concatenate([entries(a) for a in par]); v = np.concatenate([entries(a) for a in val])
    q = p
    for k in range(DEP - 1): q = p[q]
    return {"y": np.stack([np.ascontiguousarray(v[q][V * r:V * r + V].reshape(-1, 16).T) for r in range(N)])}

@@ -1,0 +1,379 @@
+import numpy as np
+from concourse.bass import DstId, RemoteDMATransfer
+from concourse.mybir import AluOpType, ActivationFunctionType
+
+N = 12
+SIM = 64
+SLOT = 4096
+WIN = 6 * SLOT
+PIECE = (6, 10)
+PCOL = (0, 192, 512)
+WORK = ((0, 0, 128, 192, 0, 6), (1, 0, 64, 160, 6, 11), (1, 64, 128, 160, 11, 16))
+HOPS = 8
+RG = 4
+BW = 768
+
+SCRATCH = {
+    "D0": ("dram", [N, 128, 192], "float32"),
+    "D1": ("dram", [N, 128, 320], "float32"),
+    "VD": ("dram", [N, 128, 512], "bfloat16"),
+    "YD": ("dram", [2, 128, 160], "bfloat16"),
+    "TAB": ("sbuf", [128, WIN], "float32"),
+    "VAL": ("sbuf", [128, WIN], "bfloat16"),
+    "PI": ("sbuf", [128, 512], "int32"),
+    "T1": ("sbuf", [128, 512], "int32"),
+    "T2": ("sbuf", [128, 512], "int32"),
+    "T3": ("sbuf", [128, 512], "int32"),
+    "CODE": ("sbuf", [128, 512], "float32"),
+    "VS": ("sbuf", [128, 512], "bfloat16"),
+    "XS": ("sbuf", [128, 192], "float32"),
+    "YS": ("sbuf", [128, 192], "bfloat16"),
+    "MW": ("sbuf", [128, 32], "bfloat16"),
+    "SH": ("sbuf", [128, 256], "float32"),
+    "BF": ("sbuf", [128, 4], "float32"),
+    "BB": ("sbuf", [128, 16], "bfloat16"),
+}
+for _c in (0, 1):
+    SCRATCH["LI%d" % _c] = ("sbuf", [128, 192], "int32")
+    SCRATCH["OA%d" % _c] = ("sbuf", [128, 192], "int32")
+    SCRATCH["RB%d" % _c] = ("sbuf", [128, 192], "int32")
+    SCRATCH["OFF%d" % _c] = ("sbuf", [128, 192], "uint16")
+    SCRATCH["ROW%d" % _c] = ("sbuf", [128, 192], "uint16")
+    SCRATCH["LP%d" % _c] = ("psum", [128, 512], "float32")
+    SCRATCH["XP%d" % _c] = ("psum", [128, 512], "float32")
+for _c in range(RG):
+    SCRATCH["MK%d" % _c] = ("sbuf", [128, BW], "bfloat16")
+    SCRATCH["G%d" % _c] = ("sbuf", [128, BW], "float32")
+    SCRATCH["GB%d" % _c] = ("sbuf", [128, BW], "bfloat16")
+
+SEMAPHORES = (["p%d_%d" % (r, h) for r in range(N) for h in (0, 1)] + ["v%d" % r for r in range(N)]
+              + ["sent", "lp0", "lp1", "lv", "ow0", "ow1", "en0", "en1", "ms", "cq", "x0", "lda", "ldb", "vl", "vq", "ys", "yo", "y1", "y2"]
+              + ["%s%d" % (s, c) for s in ("pd", "xd", "xs", "de") for c in (0, 1)]
+              + ["%s%d" % (s, c) for s in ("gs", "rs", "mk") for c in range(RG)])
+
+
+def _bits(m):
+    return bin(m).count("1")
+
+
+def _mask(topo, src, dsts):
+    m = topo.mask(src, dsts[0])
+    for d in dsts:
+        m &= topo.mask(src, d)
+    return m
+
+
+def _plan(cores, topo):
+    chips = {}
+    for c in range(SIM):
+        chips.setdefault(topo.chip(c), []).append(c)
+    homes = sorted({topo.chip(c) for c in cores})
+    mate = {h: [x for x in sorted(chips) if topo.mates(h, x)][0] for h in homes}
+    member = {}
+    for h in homes:
+        member[h] = chips[h]
+        member[mate[h]] = [c for c in chips[mate[h]] if topo.may_write(c, chips[h][0])]
+    holder, agent, magent, task = {}, {}, {}, {}
+    load = {c: 0.0 for x in member for c in member[x]}
+    for h in homes:
+        m = mate[h]
+        ranks = [r for r in range(N) if topo.chip(cores[r]) == h]
+        own_h = [c for c in chips[h] if topo.may_write(c, chips[m][0])]
+        free = [c for c in own_h if c not in cores]
+        rest = [c for c in chips[h] if c not in cores]
+        for r in ranks:
+            agent[r] = cores[r] if cores[r] in own_h else free.pop(0)
+        left = list(member[m])
+        for i, r in enumerate(ranks):
+            c = [c for c in left if topo.die(c) == topo.die(agent[r])][0]
+            left.remove(c)
+            magent[r] = c
+            holder[(h, r)], holder[(m, r)] = cores[r], c
+            load[cores[r]] += 1.0
+            load[agent[r]] += 0.5
+            load[c] += 1.0
+            task[cores[r]], task[rest[i]], task[c] = (r, 0), (r, 1), (r, 2)
+    sends = {c: [] for c in load}
+    area = {r: (topo.chip(cores[r]), mate[topo.chip(cores[r])]) for r in range(N)}
+    cls = {(x, r): 0 if x in area[r] else 1 if topo.same_plane(area[r][0], x) else 2 for r in range(N) for x in member}
+    land = {}
+    for k in (1, 2):
+        for r in range(N):
+            a = agent[r] if k == 1 else magent[r]
+            for y in sorted(member):
+                if cls[(y, r)] == k:
+                    c = min(member[y], key=lambda c: (load[c] + (0.6 if topo.die(c) != topo.die(a) else 0.0), c))
+                    load[c] += 1.0
+                    holder[(y, r)] = c
+                    land.setdefault((k, r), []).append(c)
+    for r in range(N):
+        h, root = area[r][0], cores[r]
+        if agent[r] != root:
+            sends[root].append((0, r, [agent[r]]))
+        sends[agent[r]].append((0, r, [magent[r]]))
+        sends[agent[r]].append((0, r, land[(1, r)]))
+        sends[magent[r]].append((0, r, land[(2, r)]))
+        for x in sorted(member):
+            b = holder[(x, r)]
+            sends[b].append((cls[(x, r)], r, [c for c in member[x] if c != b and not (c == agent[r] and c != root and x == h)]))
+    cnt = {}
+    for s in sends:
+        for k, r, ds in sends[s]:
+            for d in ds:
+                cnt[(d, r)] = _bits(_mask(topo, s, ds))
+    return {"task": task, "sends": sends, "cnt": cnt, "cls": cls}
+
+
+def rank_program(g, core, T, topo):
+    P = _plan(T.cores, topo)
+    if core not in P["task"]:
+        return
+    chip = topo.chip(core)
+    me = T.rank_of(core)
+    S = T.sem
+    V, A, PE, SY = g.vector, g.scalar, g.tensor, g.sync
+    Copy = ActivationFunctionType.Copy
+    cnt = {}
+
+    def inc(ins, sem, n=1):
+        ins.then_inc(S[sem], n)
+        cnt[sem] = cnt.get(sem, 0) + n
+
+    def send(src, dsts, name, idx, sem):
+        mask = _mask(topo, core, dsts)
+        ids, aps = [], []
+        for d in dsts:
+            rid, pid, _ = topo.addr(d)
+            ids.append(DstId(rid=rid, pnc=pid))
+            aps.append(T[name][idx])
+        g.remote_dma_fused([RemoteDMATransfer(dst_ids=ids, dma_engine_mask=mask, remote_sem=S[sem], srcs=[src], dsts=aps)],
+                           local_sem=S.sent)
+        cnt["sent"] = cnt.get("sent", 0) + _bits(mask)
+
+    for r in range(N):
+        if r != me:
+            n = P["cnt"][(core, r)]
+            for s in ("p%d_0", "p%d_1", "v%d"):
+                cnt[s % r] = n
+    order, vorder = [], []
+    for k in range(3):
+        rs = [r for r in range(N) if P["cls"][(chip, r)] == k]
+        rs.sort(key=lambda r: (r != me, r))
+        order += [(r, h) for h in (0, 1) for r in rs]
+        vorder += rs
+    myr, part = P["task"][core]
+    wp, wlo, whi, COLS, ylo, yhi = WORK[part]
+    NC = COLS // 2
+    NB = NC // 4
+    NS = 4
+    PB = NB // NS
+    SW = 128 * PB
+
+    inc(V.memset(T.MW[:], 0.0), "ms")
+    inc(V.memset(T.SH[:], 0.0), "ms")
+    inc(V.memset(T.BF[:], 1.0), "ms")
+    inc(V.memset(T.BB[:], 1.0), "ms")
+    g.wait_ge(S.ms, 4)
+
+    def sel(ap, pattern, op, fill, base, cm):
+        inc(g.affine_select(ap, ap, pattern, op, fill, base, cm), "cq")
+
+    ne, ge = AluOpType.not_equal, AluOpType.is_ge
+    for h in (0, 1):
+        sel(T.SH[:, 128 * h:128 * h + 128], [[-32, 4], [0, 2], [-1, 16]], ne, 1.0, -16 * h, 1)
+    for c in range(4):
+        if c:
+            g.wait_ge(S.cq, cnt["cq"])
+        sel(T.MW[:], [[-1, 32]], ne, 1.0, -32 * c, 1)
+        if c < 2:
+            for b in (T.BF[:], T.BB[:, 0:4]):
+                if c == 0:
+                    sel(b, [[-32, 4]], ge, 0.0, 0, 1)
+                else:
+                    sel(b, [[32, 4]], ge, 0.0, 31, -1)
+    NCQ = cnt["cq"]
+
+    PR = (0, PIECE[0], 16)
+    if me is not None:
+        for h in (0, 1):
+            inc(SY.dma_start(T.PI[:, PCOL[h]:PCOL[h + 1]], T.par[PR[h]:PR[h + 1], :]), "lp%d" % h, 16)
+        inc(A.dma_start(T.VS[:], T.val[:]), "lv", 16)
+        for h in (0, 1):
+            s = slice(PCOL[h], PCOL[h + 1])
+            V.wait_ge(S["lp%d" % h], 16)
+            inc(V.tensor_scalar(T.T2[:, s], T.PI[:, s], 15, None, AluOpType.bitwise_and), "vq")
+            inc(V.tensor_scalar(T.T1[:, s], T.PI[:, s], 4, None, AluOpType.logical_shift_right), "vq")
+            inc(V.tensor_scalar(T.T3[:, s], T.PI[:, s], 393216, 499712, AluOpType.is_ge, AluOpType.mult), "vq")
+            V.wait_ge(S.vq, cnt["vq"])
+            inc(V.tensor_scalar(T.T2[:, s], T.T2[:, s], 32768, None, AluOpType.mult), "vq")
+            inc(V.tensor_tensor(T.T1[:, s], T.T1[:, s], T.T3[:, s], AluOpType.add), "vq")
+            V.wait_ge(S.vq, cnt["vq"])
+            inc(V.tensor_tensor(T.CODE[:, s], T.T1[:, s], T.T2[:, s], AluOpType.add), "en%d" % h)
+        for h in (0, 1):
+            SY.wait_ge(S["en%d" % h], 1)
+            inc(SY.dma_start(T["D%d" % h][me], T.CODE[:, PCOL[h]:PCOL[h + 1]]), "ow%d" % h, 16)
+
+    def here(q, r, h):
+        if r == me:
+            q.wait_ge(S["ow%d" % h], 16)
+        else:
+            q.wait_ge(S["p%d_%d" % (r, h)], cnt["p%d_%d" % (r, h)])
+
+    sends = P["sends"][core]
+    for k in range(3):
+        for h in (0, 1):
+            last = None
+            for kk, r, ds in sends:
+                if kk != k:
+                    continue
+                if last != r:
+                    if r == me:
+                        g.wait_ge(S["en%d" % h], 1)
+                    else:
+                        here(g, r, h)
+                    last = r
+                send(T.CODE[:, PCOL[h]:PCOL[h + 1]] if r == me else T["D%d" % h][r], ds, "D%d" % h, r, "p%d_%d" % (r, h))
+    for k in range(3):
+        last = None
+        for kk, r, ds in sends:
+            if kk != k:
+                continue
+            if last != r:
+                if r == me:
+                    g.wait_ge(S.lv, 16)
+                else:
+                    g.wait_ge(S["v%d" % r], cnt["v%d" % r])
+                last = r
+            send(T.VS[:] if r == me else T.VD[r], ds, "VD", r, "v%d" % r)
+
+    def table(q, r, h, cl, sem):
+        a, slot = divmod(r, 6)
+        p0 = 32 * cl + 16 * a
+        inc(q.dma_start(T.TAB[p0 + PR[h]:p0 + PR[h + 1], SLOT * slot:SLOT * slot + SLOT], T["D%d" % h][r]), sem, 16)
+
+    for r, h in order:
+        here(SY, r, h)
+        for cl in (0, 1):
+            table(SY, r, h, cl, "lda")
+        if r == myr and h == wp:
+            inc(SY.dma_start(T.XS[:, 0:COLS], T["D%d" % h][r][wlo:whi, :]), "x0", 16)
+    for r in vorder:
+        if r != me:
+            SY.wait_ge(S["v%d" % r], cnt["v%d" % r])
+        a, slot = divmod(r, 6)
+        for cl in range(4):
+            p0 = 32 * cl + 16 * a
+            inc(SY.dma_start(T.VAL[p0:p0 + 16, SLOT * slot:SLOT * slot + SLOT], T.val[:] if r == me else T.VD[r]), "vl", 16)
+
+    steps = 2 * HOPS
+    NAREA = 2 * len([1 for r in range(N) if P["cls"][(chip, r)] == 0])
+
+    def dup(i):
+        t, c = divmod(i, 2)
+        if t:
+            PE.wait_ge(S["xs%d" % c], t)
+        for h in (0, 1):
+            inc(PE.matmul(T["LP%d" % c][:, h:2 * NC:2], T.SH[:, 128 * h:128 * h + 128], T.XS[:, NC * c:NC * c + NC], True, True), "pd%d" % c)
+
+    def dec(i):
+        t, c = divmod(i, 2)
+        V.wait_ge(S["pd%d" % c], 2 * (t + 1))
+        LI, OA, RB = T["LI%d" % c][:, 0:2 * NC], T["OA%d" % c][:, 0:2 * NC], T["RB%d" % c][:, 0:2 * NC]
+        inc(V.tensor_copy(LI, T["LP%d" % c][:, 0:2 * NC]), "vq")
+        V.wait_ge(S.vq, cnt["vq"])
+        inc(V.tensor_scalar(RB, LI, 15, None, AluOpType.logical_shift_right), "vq")
+        inc(V.tensor_scalar(OA, LI, 32767, None, AluOpType.bitwise_and), "vq")
+        V.wait_ge(S.vq, cnt["vq"])
+        inc(V.tensor_copy(T["ROW%d" % c][:, 0:2 * NC], RB), "de%d" % c)
+        inc(V.tensor_copy(T["OFF%d" % c][:, 0:2 * NC], OA), "vq")
+
+    def mask(i, s):
+        t, c = divmod(i, 2)
+        u = NS * i + s
+        if s == 0:
+            A.wait_ge(S["de%d" % c], t + 1)
+        if u >= RG:
+            A.wait_ge(S["gs%d" % (u % RG)], u // RG)
+        inc(A.activation(T["MK%d" % (u % RG)][:, 0:SW], T.MW[:].indirect(T["ROW%d" % c][:, 8 * PB * s:8 * PB * (s + 1)]), Copy),
+            "mk%d" % (u % RG))
+
+    def back(i):
+        t, c = divmod(i, 2)
+        A.wait_ge(S["xd%d" % c], NB * t)
+        if t < HOPS:
+            inc(A.activation(T.XS[:, NC * c:NC * c + NC], T["XP%d" % c][:, 0:NC], Copy), "xs%d" % c)
+        else:
+            inc(A.activation(T.YS[:, NC * c:NC * c + NC], T["XP%d" % c][:, 0:NC], Copy), "ys")
+
+    PE.wait_ge(S.cq, NCQ)
+    PE.wait_ge(S.x0, 16)
+    dup(0)
+    dup(1)
+    for i in range(steps):
+        t, c = divmod(i, 2)
+        B = T.BB[:, 0:4] if t == HOPS - 1 else T.BF[:]
+        for s in range(NS):
+            u = NS * i + s
+            G = T[("GB%d" if t == HOPS - 1 else "G%d") % (u % RG)]
+            PE.wait_ge(S["gs%d" % (u % RG)], u // RG + 1)
+            for b in range(PB):
+                o = 4 * (PB * s + b)
+                inc(PE.matmul(T["XP%d" % c][:, o:o + 4], G[:, 128 * b:128 * b + 128], B, True, True), "xd%d" % c)
+            if s == 0 and 2 <= i + 1 < steps:
+                dup(i + 1)
+
+    for j, (r, h) in enumerate(order):
+        here(A, r, h)
+        for cl in (2, 3):
+            table(A, r, h, cl, "ldb")
+        if j == NAREA - 1:
+            A.wait_ge(S.cq, NCQ)
+            for s in range(NS):
+                mask(0, s)
+    for i in range(steps):
+        for s in range(NS):
+            if i >= 1:
+                mask(i, s)
+            if s == 1 and i >= 1:
+                back(i + 1)
+    back(steps + 1)
+
+    dec(0)
+    dec(1)
+    V.wait_ge(S.lda, cnt["lda"])
+    V.wait_ge(S.ldb, cnt["ldb"])
+    for i in range(steps):
+        t, c = divmod(i, 2)
+        lastt = t == HOPS - 1
+        if lastt and c == 0:
+            V.wait_ge(S.vl, cnt["vl"])
+        W = T.VAL if lastt else T.TAB
+        for s in range(NS):
+            u = NS * i + s
+            G = T[("GB%d" if lastt else "G%d") % (u % RG)]
+            if s == 0:
+                V.wait_ge(S.vq, cnt["vq"])
+            if u >= RG:
+                V.wait_ge(S["xd%d" % (1 - c)], NB * ((i - 1) // 2) + PB * (s + 1))
+            V.wait_ge(S["mk%d" % (u % RG)], u // RG + 1)
+            inc(V.tensor_tensor(G[:, 0:SW], W[:].indirect(T["OFF%d" % c][:, 8 * PB * s:8 * PB * (s + 1)]),
+                                T["MK%d" % (u % RG)][:, 0:SW], AluOpType.mult), "gs%d" % (u % RG))
+            if s == 2 and 2 <= i + 1 < steps:
+                dec(i + 1)
+
+    if me is not None:
+        SY.wait_ge(S.ys, 2)
+        inc(SY.dma_start(T.y[ylo:yhi, :], T.YS[:, 0:COLS]), "yo", 16)
+        for c in P["task"]:
+            r, k = P["task"][c]
+            if r == me and k:
+                cnt["y%d" % k] = _bits(_mask(topo, c, [core]))
+        for k in (1, 2):
+            SY.wait_ge(S["y%d" % k], cnt["y%d" % k])
+            inc(SY.dma_start(T.y[WORK[k][4]:WORK[k][5], :], T.YD[k - 1]), "yo", 16)
+    else:
+        g.wait_ge(S.ys, 2)
+        send(T.YS[:, 0:COLS], [T.cores[myr]], "YD", part - 1, "y%d" % part)
+    for s in SEMAPHORES:
+        if cnt.get(s, 0):
+            g.wait_ge(S[s], cnt[s])

@@ -6,18 +6,22 @@ N = 12
 SIM = 64
 SLOT = 4096
 WIN = 6 * SLOT
-PIECE = (6, 10)
-PCOL = (0, 192, 512)
-WORK = ((0, 0, 128, 192, 0, 6), (1, 0, 64, 160, 6, 11), (1, 64, 128, 160, 11, 16))
+PR = (0, 10, 16)
+PCOL = (0, 320, 512)
+YROW = ((0, 5), (5, 10), (10, 15), (15, 16))
 HOPS = 8
 RG = 4
-BW = 768
+BW = 640
+NS = 4
 
 SCRATCH = {
-    "D0": ("dram", [N, 128, 192], "float32"),
-    "D1": ("dram", [N, 128, 320], "float32"),
+    "D0": ("dram", [N, 128, 320], "float32"),
+    "D1": ("dram", [N, 128, 192], "float32"),
     "VD": ("dram", [N, 128, 512], "bfloat16"),
-    "YD": ("dram", [2, 128, 160], "bfloat16"),
+    "YD1": ("dram", [128, 160], "bfloat16"),
+    "YD2": ("dram", [128, 160], "bfloat16"),
+    "YD3": ("dram", [128, 32], "bfloat16"),
+    "FW": ("sbuf", [128, 128], "bfloat16"),
     "TAB": ("sbuf", [128, WIN], "float32"),
     "VAL": ("sbuf", [128, WIN], "bfloat16"),
     "PI": ("sbuf", [128, 512], "int32"),
@@ -26,19 +30,19 @@ SCRATCH = {
     "T3": ("sbuf", [128, 512], "int32"),
     "CODE": ("sbuf", [128, 512], "float32"),
     "VS": ("sbuf", [128, 512], "bfloat16"),
-    "XS": ("sbuf", [128, 192], "float32"),
-    "YS": ("sbuf", [128, 192], "bfloat16"),
+    "XS": ("sbuf", [128, 160], "float32"),
+    "YS": ("sbuf", [128, 160], "bfloat16"),
     "MW": ("sbuf", [128, 32], "bfloat16"),
     "SH": ("sbuf", [128, 256], "float32"),
     "BF": ("sbuf", [128, 4], "float32"),
     "BB": ("sbuf", [128, 16], "bfloat16"),
 }
 for _c in (0, 1):
-    SCRATCH["LI%d" % _c] = ("sbuf", [128, 192], "int32")
-    SCRATCH["OA%d" % _c] = ("sbuf", [128, 192], "int32")
-    SCRATCH["RB%d" % _c] = ("sbuf", [128, 192], "int32")
-    SCRATCH["OFF%d" % _c] = ("sbuf", [128, 192], "uint16")
-    SCRATCH["ROW%d" % _c] = ("sbuf", [128, 192], "uint16")
+    SCRATCH["LI%d" % _c] = ("sbuf", [128, 160], "int32")
+    SCRATCH["OA%d" % _c] = ("sbuf", [128, 160], "int32")
+    SCRATCH["RB%d" % _c] = ("sbuf", [128, 160], "int32")
+    SCRATCH["OFF%d" % _c] = ("sbuf", [128, 160], "uint16")
+    SCRATCH["ROW%d" % _c] = ("sbuf", [128, 160], "uint16")
     SCRATCH["LP%d" % _c] = ("psum", [128, 512], "float32")
     SCRATCH["XP%d" % _c] = ("psum", [128, 512], "float32")
 for _c in range(RG):
@@ -47,9 +51,9 @@ for _c in range(RG):
     SCRATCH["GB%d" % _c] = ("sbuf", [128, BW], "bfloat16")
 
 SEMAPHORES = (["p%d_%d" % (r, h) for r in range(N) for h in (0, 1)] + ["v%d" % r for r in range(N)]
-              + ["sent", "lp0", "lp1", "lv", "ow0", "ow1", "en0", "en1", "ms", "cq", "x0", "lda", "ldb", "vl", "vq", "ys", "yo", "y1", "y2"]
+              + ["sent", "lp0", "lp1", "lv", "ow0", "ow1", "en0", "en1", "ms", "cq", "x0", "lda", "ldb", "vl", "vq", "ys", "yo", "y1", "y2", "y3", "fw"]
               + ["%s%d" % (s, c) for s in ("pd", "xd", "xs", "de") for c in (0, 1)]
-              + ["%s%d" % (s, c) for s in ("gs", "rs", "mk") for c in range(RG)])
+              + ["%s%d" % (s, c) for s in ("gs", "mk") for c in range(RG)])
 
 
 def _bits(m):
@@ -69,10 +73,14 @@ def _plan(cores, topo):
         chips.setdefault(topo.chip(c), []).append(c)
     homes = sorted({topo.chip(c) for c in cores})
     mate = {h: [x for x in sorted(chips) if topo.mates(h, x)][0] for h in homes}
-    member = {}
+    member, via = {}, {}
     for h in homes:
+        m = mate[h]
+        own = [c for c in chips[m] if topo.may_write(c, chips[h][0])]
+        extra = [c for c in chips[m] if c not in own][0]
+        via[extra] = [c for c in own if topo.die(c) == topo.die(extra)][0]
         member[h] = chips[h]
-        member[mate[h]] = [c for c in chips[mate[h]] if topo.may_write(c, chips[h][0])]
+        member[m] = own + [extra]
     holder, agent, magent, task = {}, {}, {}, {}
     load = {c: 0.0 for x in member for c in member[x]}
     for h in homes:
@@ -83,7 +91,8 @@ def _plan(cores, topo):
         rest = [c for c in chips[h] if c not in cores]
         for r in ranks:
             agent[r] = cores[r] if cores[r] in own_h else free.pop(0)
-        left = list(member[m])
+        left = member[m][:-1]
+        task[member[m][-1]] = (ranks, 3)
         for i, r in enumerate(ranks):
             c = [c for c in left if topo.die(c) == topo.die(agent[r])][0]
             left.remove(c)
@@ -92,7 +101,7 @@ def _plan(cores, topo):
             load[cores[r]] += 1.0
             load[agent[r]] += 0.5
             load[c] += 1.0
-            task[cores[r]], task[rest[i]], task[c] = (r, 0), (r, 1), (r, 2)
+            task[cores[r]], task[rest[i]], task[c] = ([r], 0), ([r], 1), ([r], 2)
     sends = {c: [] for c in load}
     area = {r: (topo.chip(cores[r]), mate[topo.chip(cores[r])]) for r in range(N)}
     cls = {(x, r): 0 if x in area[r] else 1 if topo.same_plane(area[r][0], x) else 2 for r in range(N) for x in member}
@@ -121,7 +130,7 @@ def _plan(cores, topo):
         for k, r, ds in sends[s]:
             for d in ds:
                 cnt[(d, r)] = _bits(_mask(topo, s, ds))
-    return {"task": task, "sends": sends, "cnt": cnt, "cls": cls}
+    return {"task": task, "sends": sends, "cnt": cnt, "cls": cls, "via": via}
 
 
 def rank_program(g, core, T, topo):
@@ -139,14 +148,13 @@ def rank_program(g, core, T, topo):
         ins.then_inc(S[sem], n)
         cnt[sem] = cnt.get(sem, 0) + n
 
-    def send(src, dsts, name, idx, sem):
+    def send(src, dsts, dst, sem):
         mask = _mask(topo, core, dsts)
-        ids, aps = [], []
+        ids = []
         for d in dsts:
             rid, pid, _ = topo.addr(d)
             ids.append(DstId(rid=rid, pnc=pid))
-            aps.append(T[name][idx])
-        g.remote_dma_fused([RemoteDMATransfer(dst_ids=ids, dma_engine_mask=mask, remote_sem=S[sem], srcs=[src], dsts=aps)],
+        g.remote_dma_fused([RemoteDMATransfer(dst_ids=ids, dma_engine_mask=mask, remote_sem=S[sem], srcs=[src], dsts=[dst for d in dsts])],
                            local_sem=S.sent)
         cnt["sent"] = cnt.get("sent", 0) + _bits(mask)
 
@@ -161,11 +169,10 @@ def rank_program(g, core, T, topo):
         rs.sort(key=lambda r: (r != me, r))
         order += [(r, h) for h in (0, 1) for r in rs]
         vorder += rs
-    myr, part = P["task"][core]
-    wp, wlo, whi, COLS, ylo, yhi = WORK[part]
+    mine, part = P["task"][core]
+    COLS = 32 * len(mine) * (YROW[part][1] - YROW[part][0])
     NC = COLS // 2
     NB = NC // 4
-    NS = 4
     PB = NB // NS
     SW = 128 * PB
 
@@ -193,7 +200,6 @@ def rank_program(g, core, T, topo):
                     sel(b, [[32, 4]], ge, 0.0, 31, -1)
     NCQ = cnt["cq"]
 
-    PR = (0, PIECE[0], 16)
     if me is not None:
         for h in (0, 1):
             inc(SY.dma_start(T.PI[:, PCOL[h]:PCOL[h + 1]], T.par[PR[h]:PR[h + 1], :]), "lp%d" % h, 16)
@@ -219,44 +225,31 @@ def rank_program(g, core, T, topo):
         else:
             q.wait_ge(S["p%d_%d" % (r, h)], cnt["p%d_%d" % (r, h)])
 
-    sends = P["sends"][core]
-    for k in range(3):
-        for h in (0, 1):
-            last = None
-            for kk, r, ds in sends:
-                if kk != k:
-                    continue
-                if last != r:
-                    if r == me:
-                        g.wait_ge(S["en%d" % h], 1)
-                    else:
-                        here(g, r, h)
-                    last = r
-                send(T.CODE[:, PCOL[h]:PCOL[h + 1]] if r == me else T["D%d" % h][r], ds, "D%d" % h, r, "p%d_%d" % (r, h))
-    for k in range(3):
-        last = None
-        for kk, r, ds in sends:
-            if kk != k:
-                continue
-            if last != r:
-                if r == me:
-                    g.wait_ge(S.lv, 16)
-                else:
-                    g.wait_ge(S["v%d" % r], cnt["v%d" % r])
-                last = r
-            send(T.VS[:] if r == me else T.VD[r], ds, "VD", r, "v%d" % r)
-
     def table(q, r, h, cl, sem):
         a, slot = divmod(r, 6)
         p0 = 32 * cl + 16 * a
         inc(q.dma_start(T.TAB[p0 + PR[h]:p0 + PR[h + 1], SLOT * slot:SLOT * slot + SLOT], T["D%d" % h][r]), sem, 16)
 
+    def first(out, in_):
+        inc(SY.dma_start(out, in_), "x0", 16)
+
     for r, h in order:
         here(SY, r, h)
         for cl in (0, 1):
             table(SY, r, h, cl, "lda")
-        if r == myr and h == wp:
-            inc(SY.dma_start(T.XS[:, 0:COLS], T["D%d" % h][r][wlo:whi, :]), "x0", 16)
+        if r in mine and h == (0, 0, 1, 1)[part]:
+            D = T["D%d" % h][r]
+            if part < 2:
+                first(T.XS[:, 0:160], D[64 * part:64 * part + 64, :])
+            elif part == 2:
+                first(T.XS[0:126, 0:160], D[0:105, :])
+                first(T.XS[126:127, 0:160], D[105:106, 0:160])
+                first(T.XS[127:128, 0:32], D[105:106, 160:192])
+                first(T.XS[127:128, 32:160], D[106:107, 0:128])
+            else:
+                k = 32 * mine.index(r)
+                first(T.XS[0:2, k:k + 32], D[106:107, 128:192])
+                first(T.XS[2:128, k:k + 32], D[107:128, :])
     for r in vorder:
         if r != me:
             SY.wait_ge(S["v%d" % r], cnt["v%d" % r])
@@ -306,7 +299,7 @@ def rank_program(g, core, T, topo):
             inc(A.activation(T.YS[:, NC * c:NC * c + NC], T["XP%d" % c][:, 0:NC], Copy), "ys")
 
     PE.wait_ge(S.cq, NCQ)
-    PE.wait_ge(S.x0, 16)
+    PE.wait_ge(S.x0, cnt["x0"])
     dup(0)
     dup(1)
     for i in range(steps):
@@ -361,19 +354,57 @@ def rank_program(g, core, T, topo):
             if s == 2 and 2 <= i + 1 < steps:
                 dec(i + 1)
 
+    sends = P["sends"][core]
+    for k in range(3):
+        for h in (0, 1):
+            last = None
+            for kk, r, ds in sends:
+                if kk != k:
+                    continue
+                if last != r:
+                    if r == me:
+                        g.wait_ge(S["en%d" % h], 1)
+                    else:
+                        here(g, r, h)
+                    last = r
+                send(T.CODE[:, PCOL[h]:PCOL[h + 1]] if r == me else T["D%d" % h][r], ds, T["D%d" % h][r], "p%d_%d" % (r, h))
+    g.wait_ge(S.lda, cnt["lda"])
+    g.wait_ge(S.ldb, cnt["ldb"])
+    for k in range(3):
+        last = None
+        for kk, r, ds in sends:
+            if kk != k:
+                continue
+            if last != r:
+                if r == me:
+                    g.wait_ge(S.lv, 16)
+                else:
+                    g.wait_ge(S["v%d" % r], cnt["v%d" % r])
+                last = r
+            send(T.VS[:] if r == me else T.VD[r], ds, T.VD[r], "v%d" % r)
+
+    for e in P["via"]:
+        if P["via"][e] == core:
+            cnt["fw"] = _bits(_mask(topo, e, [core]))
+            g.wait_ge(S.fw, cnt["fw"])
+            for i, r in enumerate(P["task"][e][0]):
+                send(T.FW[:, 32 * i:32 * i + 32], [T.cores[r]], T.YD3[:], "y3")
     if me is not None:
         SY.wait_ge(S.ys, 2)
-        inc(SY.dma_start(T.y[ylo:yhi, :], T.YS[:, 0:COLS]), "yo", 16)
+        inc(SY.dma_start(T.y[0:5, :], T.YS[:]), "yo", 16)
         for c in P["task"]:
-            r, k = P["task"][c]
-            if r == me and k:
-                cnt["y%d" % k] = _bits(_mask(topo, c, [core]))
-        for k in (1, 2):
+            rs, k = P["task"][c]
+            if me in rs and k:
+                cnt["y%d" % k] = _bits(_mask(topo, P["via"].get(c, c), [core]))
+        for k in (3, 1, 2):
             SY.wait_ge(S["y%d" % k], cnt["y%d" % k])
-            inc(SY.dma_start(T.y[WORK[k][4]:WORK[k][5], :], T.YD[k - 1]), "yo", 16)
+            inc(SY.dma_start(T.y[YROW[k][0]:YROW[k][1], :], T["YD%d" % k][:]), "yo", 16)
     else:
         g.wait_ge(S.ys, 2)
-        send(T.YS[:, 0:COLS], [T.cores[myr]], "YD", part - 1, "y%d" % part)
+        if part == 3:
+            send(T.YS[:, 0:128], [P["via"][core]], T.FW[:], "fw")
+        else:
+            send(T.YS[:], [T.cores[mine[0]]], T["YD%d" % part][:], "y%d" % part)
     for s in SEMAPHORES:
         if cnt.get(s, 0):
             g.wait_ge(S[s], cnt[s])

import numpy as np
from concourse.bass import DstId, RemoteDMATransfer
from concourse.mybir import AluOpType, ActivationFunctionType

N = 12
SIM = 64
SLOT = 4096
WIN = 6 * SLOT
PR = (0, 10, 16)
PCOL = (0, 320, 512)
YROW = ((0, 5), (5, 10), (10, 15), (15, 16))
HOPS = 8
RG = 4
BW = 640
NS = 4

SCRATCH = {
    "D0": ("dram", [N, 128, 320], "float32"),
    "D1": ("dram", [N, 128, 192], "float32"),
    "VD": ("dram", [N, 128, 512], "bfloat16"),
    "YD1": ("dram", [128, 160], "bfloat16"),
    "YD2": ("dram", [128, 160], "bfloat16"),
    "YD3": ("dram", [128, 32], "bfloat16"),
    "FW": ("sbuf", [128, 128], "bfloat16"),
    "TAB": ("sbuf", [128, WIN], "float32"),
    "VAL": ("sbuf", [128, WIN], "bfloat16"),
    "PI": ("sbuf", [128, 512], "int32"),
    "T1": ("sbuf", [128, 512], "int32"),
    "T2": ("sbuf", [128, 512], "int32"),
    "T3": ("sbuf", [128, 512], "int32"),
    "CODE": ("sbuf", [128, 512], "float32"),
    "VS": ("sbuf", [128, 512], "bfloat16"),
    "XS": ("sbuf", [128, 160], "float32"),
    "YS": ("sbuf", [128, 160], "bfloat16"),
    "MW": ("sbuf", [128, 32], "bfloat16"),
    "SH": ("sbuf", [128, 256], "float32"),
    "BF": ("sbuf", [128, 4], "float32"),
    "BB": ("sbuf", [128, 16], "bfloat16"),
}
for _c in (0, 1):
    SCRATCH["LI%d" % _c] = ("sbuf", [128, 160], "int32")
    SCRATCH["OA%d" % _c] = ("sbuf", [128, 160], "int32")
    SCRATCH["RB%d" % _c] = ("sbuf", [128, 160], "int32")
    SCRATCH["OFF%d" % _c] = ("sbuf", [128, 160], "uint16")
    SCRATCH["ROW%d" % _c] = ("sbuf", [128, 160], "uint16")
    SCRATCH["LP%d" % _c] = ("psum", [128, 512], "float32")
    SCRATCH["XP%d" % _c] = ("psum", [128, 512], "float32")
for _c in range(RG):
    SCRATCH["MK%d" % _c] = ("sbuf", [128, BW], "bfloat16")
    SCRATCH["G%d" % _c] = ("sbuf", [128, BW], "float32")
    SCRATCH["GB%d" % _c] = ("sbuf", [128, BW], "bfloat16")

SEMAPHORES = (["p%d_%d" % (r, h) for r in range(N) for h in (0, 1)] + ["v%d" % r for r in range(N)]
              + ["sent", "lp0", "lp1", "lv", "ow0", "ow1", "en0", "en1", "ms", "cq", "x0", "lda", "ldb", "vl", "vq", "ys", "yo", "y1", "y2", "y3", "fw"]
              + ["%s%d" % (s, c) for s in ("pd", "xd", "xs", "de") for c in (0, 1)]
              + ["%s%d" % (s, c) for s in ("gs", "mk") for c in range(RG)])


def _bits(m):
    return bin(m).count("1")


def _mask(topo, src, dsts):
    m = topo.mask(src, dsts[0])
    for d in dsts:
        m &= topo.mask(src, d)
    return m


def _plan(cores, topo):
    chips = {}
    for c in range(SIM):
        chips.setdefault(topo.chip(c), []).append(c)
    homes = sorted({topo.chip(c) for c in cores})
    mate = {h: [x for x in sorted(chips) if topo.mates(h, x)][0] for h in homes}
    member, via = {}, {}
    for h in homes:
        m = mate[h]
        own = [c for c in chips[m] if topo.may_write(c, chips[h][0])]
        extra = [c for c in chips[m] if c not in own][0]
        via[extra] = [c for c in own if topo.die(c) == topo.die(extra)][0]
        member[h] = chips[h]
        member[m] = own + [extra]
    holder, agent, magent, task = {}, {}, {}, {}
    load = {c: 0.0 for x in member for c in member[x]}
    for h in homes:
        m = mate[h]
        ranks = [r for r in range(N) if topo.chip(cores[r]) == h]
        own_h = [c for c in chips[h] if topo.may_write(c, chips[m][0])]
        free = [c for c in own_h if c not in cores]
        rest = [c for c in chips[h] if c not in cores]
        for r in ranks:
            agent[r] = cores[r] if cores[r] in own_h else free.pop(0)
        left = member[m][:-1]
        task[member[m][-1]] = (ranks, 3)
        for i, r in enumerate(ranks):
            c = [c for c in left if topo.die(c) == topo.die(agent[r])][0]
            left.remove(c)
            magent[r] = c
            holder[(h, r)], holder[(m, r)] = cores[r], c
            load[cores[r]] += 1.0
            load[agent[r]] += 0.5
            load[c] += 1.0
            task[cores[r]], task[rest[i]], task[c] = ([r], 0), ([r], 1), ([r], 2)
    sends = {c: [] for c in load}
    area = {r: (topo.chip(cores[r]), mate[topo.chip(cores[r])]) for r in range(N)}
    cls = {(x, r): 0 if x in area[r] else 1 if topo.same_plane(area[r][0], x) else 2 for r in range(N) for x in member}
    land = {}
    for k in (1, 2):
        for r in range(N):
            a = agent[r] if k == 1 else magent[r]
            for y in sorted(member):
                if cls[(y, r)] == k:
                    c = min(member[y], key=lambda c: (load[c] + (0.6 if topo.die(c) != topo.die(a) else 0.0), c))
                    load[c] += 1.0
                    holder[(y, r)] = c
                    land.setdefault((k, r), []).append(c)
    for r in range(N):
        h, root = area[r][0], cores[r]
        if agent[r] != root:
            sends[root].append((0, r, [agent[r]]))
        sends[agent[r]].append((0, r, [magent[r]]))
        sends[agent[r]].append((0, r, land[(1, r)]))
        sends[magent[r]].append((0, r, land[(2, r)]))
        for x in sorted(member):
            b = holder[(x, r)]
            sends[b].append((cls[(x, r)], r, [c for c in member[x] if c != b and not (c == agent[r] and c != root and x == h)]))
    cnt = {}
    for s in sends:
        for k, r, ds in sends[s]:
            for d in ds:
                cnt[(d, r)] = _bits(_mask(topo, s, ds))
    return {"task": task, "sends": sends, "cnt": cnt, "cls": cls, "via": via}


def rank_program(g, core, T, topo):
    P = _plan(T.cores, topo)
    if core not in P["task"]:
        return
    chip = topo.chip(core)
    me = T.rank_of(core)
    S = T.sem
    V, A, PE, SY = g.vector, g.scalar, g.tensor, g.sync
    Copy = ActivationFunctionType.Copy
    cnt = {}

    def inc(ins, sem, n=1):
        ins.then_inc(S[sem], n)
        cnt[sem] = cnt.get(sem, 0) + n

    def send(src, dsts, dst, sem):
        mask = _mask(topo, core, dsts)
        ids = []
        for d in dsts:
            rid, pid, _ = topo.addr(d)
            ids.append(DstId(rid=rid, pnc=pid))
        g.remote_dma_fused([RemoteDMATransfer(dst_ids=ids, dma_engine_mask=mask, remote_sem=S[sem], srcs=[src], dsts=[dst for d in dsts])],
                           local_sem=S.sent)
        cnt["sent"] = cnt.get("sent", 0) + _bits(mask)

    for r in range(N):
        if r != me:
            n = P["cnt"][(core, r)]
            for s in ("p%d_0", "p%d_1", "v%d"):
                cnt[s % r] = n
    order, vorder = [], []
    for k in range(3):
        rs = [r for r in range(N) if P["cls"][(chip, r)] == k]
        rs.sort(key=lambda r: (r != me, r))
        order += [(r, h) for h in (0, 1) for r in rs]
        vorder += rs
    mine, part = P["task"][core]
    COLS = 32 * len(mine) * (YROW[part][1] - YROW[part][0])
    NC = COLS // 2
    NB = NC // 4
    PB = NB // NS
    SW = 128 * PB

    inc(V.memset(T.MW[:], 0.0), "ms")
    inc(V.memset(T.SH[:], 0.0), "ms")
    inc(V.memset(T.BF[:], 1.0), "ms")
    inc(V.memset(T.BB[:], 1.0), "ms")
    g.wait_ge(S.ms, 4)

    def sel(ap, pattern, op, fill, base, cm):
        inc(g.affine_select(ap, ap, pattern, op, fill, base, cm), "cq")

    ne, ge = AluOpType.not_equal, AluOpType.is_ge
    for h in (0, 1):
        sel(T.SH[:, 128 * h:128 * h + 128], [[-32, 4], [0, 2], [-1, 16]], ne, 1.0, -16 * h, 1)
    for c in range(4):
        if c:
            g.wait_ge(S.cq, cnt["cq"])
        sel(T.MW[:], [[-1, 32]], ne, 1.0, -32 * c, 1)
        if c < 2:
            for b in (T.BF[:], T.BB[:, 0:4]):
                if c == 0:
                    sel(b, [[-32, 4]], ge, 0.0, 0, 1)
                else:
                    sel(b, [[32, 4]], ge, 0.0, 31, -1)
    NCQ = cnt["cq"]

    if me is not None:
        for h in (0, 1):
            inc(SY.dma_start(T.PI[:, PCOL[h]:PCOL[h + 1]], T.par[PR[h]:PR[h + 1], :]), "lp%d" % h, 16)
        inc(A.dma_start(T.VS[:], T.val[:]), "lv", 16)
        for h in (0, 1):
            s = slice(PCOL[h], PCOL[h + 1])
            V.wait_ge(S["lp%d" % h], 16)
            inc(V.tensor_scalar(T.T2[:, s], T.PI[:, s], 15, None, AluOpType.bitwise_and), "vq")
            inc(V.tensor_scalar(T.T1[:, s], T.PI[:, s], 4, None, AluOpType.logical_shift_right), "vq")
            inc(V.tensor_scalar(T.T3[:, s], T.PI[:, s], 393216, 499712, AluOpType.is_ge, AluOpType.mult), "vq")
            V.wait_ge(S.vq, cnt["vq"])
            inc(V.tensor_scalar(T.T2[:, s], T.T2[:, s], 32768, None, AluOpType.mult), "vq")
            inc(V.tensor_tensor(T.T1[:, s], T.T1[:, s], T.T3[:, s], AluOpType.add), "vq")
            V.wait_ge(S.vq, cnt["vq"])
            inc(V.tensor_tensor(T.CODE[:, s], T.T1[:, s], T.T2[:, s], AluOpType.add), "en%d" % h)
        for h in (0, 1):
            SY.wait_ge(S["en%d" % h], 1)
            inc(SY.dma_start(T["D%d" % h][me], T.CODE[:, PCOL[h]:PCOL[h + 1]]), "ow%d" % h, 16)

    def here(q, r, h):
        if r == me:
            q.wait_ge(S["ow%d" % h], 16)
        else:
            q.wait_ge(S["p%d_%d" % (r, h)], cnt["p%d_%d" % (r, h)])

    def table(q, r, h, cl, sem):
        a, slot = divmod(r, 6)
        p0 = 32 * cl + 16 * a
        inc(q.dma_start(T.TAB[p0 + PR[h]:p0 + PR[h + 1], SLOT * slot:SLOT * slot + SLOT], T["D%d" % h][r]), sem, 16)

    def first(out, in_):
        inc(SY.dma_start(out, in_), "x0", 16)

    for r, h in order:
        here(SY, r, h)
        for cl in (0, 1):
            table(SY, r, h, cl, "lda")
        if r in mine and h == (0, 0, 1, 1)[part]:
            D = T["D%d" % h][r]
            if part < 2:
                first(T.XS[:, 0:160], D[64 * part:64 * part + 64, :])
            elif part == 2:
                first(T.XS[0:126, 0:160], D[0:105, :])
                first(T.XS[126:127, 0:160], D[105:106, 0:160])
                first(T.XS[127:128, 0:32], D[105:106, 160:192])
                first(T.XS[127:128, 32:160], D[106:107, 0:128])
            else:
                k = 32 * mine.index(r)
                first(T.XS[0:2, k:k + 32], D[106:107, 128:192])
                first(T.XS[2:128, k:k + 32], D[107:128, :])
    for r in vorder:
        if r != me:
            SY.wait_ge(S["v%d" % r], cnt["v%d" % r])
        a, slot = divmod(r, 6)
        for cl in range(4):
            p0 = 32 * cl + 16 * a
            inc(SY.dma_start(T.VAL[p0:p0 + 16, SLOT * slot:SLOT * slot + SLOT], T.val[:] if r == me else T.VD[r]), "vl", 16)

    steps = 2 * HOPS
    NAREA = 2 * len([1 for r in range(N) if P["cls"][(chip, r)] == 0])

    def dup(i):
        t, c = divmod(i, 2)
        if t:
            PE.wait_ge(S["xs%d" % c], t)
        for h in (0, 1):
            inc(PE.matmul(T["LP%d" % c][:, h:2 * NC:2], T.SH[:, 128 * h:128 * h + 128], T.XS[:, NC * c:NC * c + NC], True, True), "pd%d" % c)

    def dec(i):
        t, c = divmod(i, 2)
        V.wait_ge(S["pd%d" % c], 2 * (t + 1))
        LI, OA, RB = T["LI%d" % c][:, 0:2 * NC], T["OA%d" % c][:, 0:2 * NC], T["RB%d" % c][:, 0:2 * NC]
        inc(V.tensor_copy(LI, T["LP%d" % c][:, 0:2 * NC]), "vq")
        V.wait_ge(S.vq, cnt["vq"])
        inc(V.tensor_scalar(RB, LI, 15, None, AluOpType.logical_shift_right), "vq")
        inc(V.tensor_scalar(OA, LI, 32767, None, AluOpType.bitwise_and), "vq")
        V.wait_ge(S.vq, cnt["vq"])
        inc(V.tensor_copy(T["ROW%d" % c][:, 0:2 * NC], RB), "de%d" % c)
        inc(V.tensor_copy(T["OFF%d" % c][:, 0:2 * NC], OA), "vq")

    def mask(i, s):
        t, c = divmod(i, 2)
        u = NS * i + s
        if s == 0:
            A.wait_ge(S["de%d" % c], t + 1)
        if u >= RG:
            A.wait_ge(S["gs%d" % (u % RG)], u // RG)
        inc(A.activation(T["MK%d" % (u % RG)][:, 0:SW], T.MW[:].indirect(T["ROW%d" % c][:, 8 * PB * s:8 * PB * (s + 1)]), Copy),
            "mk%d" % (u % RG))

    def back(i):
        t, c = divmod(i, 2)
        A.wait_ge(S["xd%d" % c], NB * t)
        if t < HOPS:
            inc(A.activation(T.XS[:, NC * c:NC * c + NC], T["XP%d" % c][:, 0:NC], Copy), "xs%d" % c)
        else:
            inc(A.activation(T.YS[:, NC * c:NC * c + NC], T["XP%d" % c][:, 0:NC], Copy), "ys")

    PE.wait_ge(S.cq, NCQ)
    PE.wait_ge(S.x0, cnt["x0"])
    dup(0)
    dup(1)
    for i in range(steps):
        t, c = divmod(i, 2)
        B = T.BB[:, 0:4] if t == HOPS - 1 else T.BF[:]
        for s in range(NS):
            u = NS * i + s
            G = T[("GB%d" if t == HOPS - 1 else "G%d") % (u % RG)]
            PE.wait_ge(S["gs%d" % (u % RG)], u // RG + 1)
            for b in range(PB):
                o = 4 * (PB * s + b)
                inc(PE.matmul(T["XP%d" % c][:, o:o + 4], G[:, 128 * b:128 * b + 128], B, True, True), "xd%d" % c)
            if s == 0 and 2 <= i + 1 < steps:
                dup(i + 1)

    for j, (r, h) in enumerate(order):
        here(A, r, h)
        for cl in (2, 3):
            table(A, r, h, cl, "ldb")
        if j == NAREA - 1:
            A.wait_ge(S.cq, NCQ)
            for s in range(NS):
                mask(0, s)
    for i in range(steps):
        for s in range(NS):
            if i >= 1:
                mask(i, s)
            if s == 1 and i >= 1:
                back(i + 1)
    back(steps + 1)

    dec(0)
    dec(1)
    V.wait_ge(S.lda, cnt["lda"])
    V.wait_ge(S.ldb, cnt["ldb"])
    for i in range(steps):
        t, c = divmod(i, 2)
        lastt = t == HOPS - 1
        if lastt and c == 0:
            V.wait_ge(S.vl, cnt["vl"])
        W = T.VAL if lastt else T.TAB
        for s in range(NS):
            u = NS * i + s
            G = T[("GB%d" if lastt else "G%d") % (u % RG)]
            if s == 0:
                V.wait_ge(S.vq, cnt["vq"])
            if u >= RG:
                V.wait_ge(S["xd%d" % (1 - c)], NB * ((i - 1) // 2) + PB * (s + 1))
            V.wait_ge(S["mk%d" % (u % RG)], u // RG + 1)
            inc(V.tensor_tensor(G[:, 0:SW], W[:].indirect(T["OFF%d" % c][:, 8 * PB * s:8 * PB * (s + 1)]),
                                T["MK%d" % (u % RG)][:, 0:SW], AluOpType.mult), "gs%d" % (u % RG))
            if s == 2 and 2 <= i + 1 < steps:
                dec(i + 1)

    sends = P["sends"][core]
    for k in range(3):
        for h in (0, 1):
            last = None
            for kk, r, ds in sends:
                if kk != k:
                    continue
                if last != r:
                    if r == me:
                        g.wait_ge(S["en%d" % h], 1)
                    else:
                        here(g, r, h)
                    last = r
                send(T.CODE[:, PCOL[h]:PCOL[h + 1]] if r == me else T["D%d" % h][r], ds, T["D%d" % h][r], "p%d_%d" % (r, h))
    g.wait_ge(S.lda, cnt["lda"])
    g.wait_ge(S.ldb, cnt["ldb"])
    for k in range(3):
        last = None
        for kk, r, ds in sends:
            if kk != k:
                continue
            if last != r:
                if r == me:
                    g.wait_ge(S.lv, 16)
                else:
                    g.wait_ge(S["v%d" % r], cnt["v%d" % r])
                last = r
            send(T.VS[:] if r == me else T.VD[r], ds, T.VD[r], "v%d" % r)

    for e in P["via"]:
        if P["via"][e] == core:
            cnt["fw"] = _bits(_mask(topo, e, [core]))
            g.wait_ge(S.fw, cnt["fw"])
            for i, r in enumerate(P["task"][e][0]):
                send(T.FW[:, 32 * i:32 * i + 32], [T.cores[r]], T.YD3[:], "y3")
    if me is not None:
        SY.wait_ge(S.ys, 2)
        inc(SY.dma_start(T.y[0:5, :], T.YS[:]), "yo", 16)
        for c in P["task"]:
            rs, k = P["task"][c]
            if me in rs and k:
                cnt["y%d" % k] = _bits(_mask(topo, P["via"].get(c, c), [core]))
        for k in (3, 1, 2):
            SY.wait_ge(S["y%d" % k], cnt["y%d" % k])
            inc(SY.dma_start(T.y[YROW[k][0]:YROW[k][1], :], T["YD%d" % k][:]), "yo", 16)
    else:
        g.wait_ge(S.ys, 2)
        if part == 3:
            send(T.YS[:, 0:128], [P["via"][core]], T.FW[:], "fw")
        else:
            send(T.YS[:], [T.cores[mine[0]]], T["YD%d" % part][:], "y%d" % part)
    for s in SEMAPHORES:
        if cnt.get(s, 0):
            g.wait_ge(S[s], cnt[s])
